import numpy as np
import ml_dtypes


def mxq(x, axis, fmt="e4m3"):
    dtype, down = {"e4m3": (ml_dtypes.float8_e4m3fn, 7), "e5m2": (ml_dtypes.float8_e5m2, 14)}[fmt]
    v = np.moveaxis(np.asarray(x, np.float32).astype(ml_dtypes.bfloat16).astype(np.float64), axis, -1)
    blocks = v.reshape(v.shape[:-1] + (-1, 32))
    amax = np.abs(blocks).max(-1, keepdims=True)
    byte = np.maximum(np.where(amax > 0, np.frexp(amax)[1] - 1 + 127, 0) - down, 1)
    scale = np.exp2(byte - 127.0)
    codes = (blocks / scale).astype(np.float32).astype(dtype).astype(np.float64)
    return np.moveaxis((codes * scale).reshape(v.shape), -1, axis)


WIDE = False


def mx_kscale(k):
    if not WIDE:
        return np.ones(k)
    levels = np.array([10, -10, 5, -5, 0])
    if k % 512:
        return np.exp2(np.random.permutation(np.resize(levels, k // 32))).repeat(32)
    a = np.empty((k // 512, 16))
    for p in range(k // 512):
        a[p, :8] = np.random.permutation(np.resize(levels, 8))
        for g in range(8):
            far = levels[np.abs(levels - a[p, g]) >= 10]
            a[p, g + 8] = far[np.random.randint(len(far))]
    return np.exp2(a.ravel()).repeat(32)


def f64(x):
    return np.asarray(x).astype(np.float64)


def split(x):
    m, e = np.frexp(f64(x))
    hi = np.ldexp(np.trunc(16.0 * m) / 16.0, e)
    return hi, f64(x) - hi


K, M, T = 1024, 1024, 1024


def setup_inputs():
    n = np.random.standard_normal
    s = mx_kscale(K)[:, None]
    return {
        "w": (n((K, M)) / np.sqrt(K) / s).astype(np.float32),
        "x": (n((K, T)) * s).astype(np.float32),
        "b": (0.3 * n(1024)).astype(np.float32),
    }


def reference(w, x, b):
    w_hi, w_lo = split(w)
    w_hi_, w_lo_ = mxq(w_hi, 0, "e4m3"), mxq(w_lo, 0, "e4m3")
    x_ = mxq(f64(x), 0, "e4m3")
    y = w_hi_.T @ x_ + w_lo_.T @ x_
    return y + f64(b)[:, None]

@@ -1,0 +1,193 @@
+from contextlib import ExitStack
+
+import concourse.mybir as mybir
+
+F32 = mybir.dt.float32
+BF16 = mybir.dt.bfloat16
+I32 = mybir.dt.int32
+U32 = mybir.dt.uint32
+U8 = mybir.dt.uint8
+FP8X4 = mybir.dt.float8_e4m3fn_x4
+ALU = mybir.AluOpType
+ACT = mybir.ActivationFunctionType
+
+FLOPS = 2 * 2 * 1024 * 1024 * 1024
+
+P = 128
+K_PASS = 512
+N_T = 512
+MASK = 0xFFF0FFF0 - (1 << 32)
+
+LOADS = [
+    ("w", 0, 0, 2), ("x", 0, 0, 1), ("w", 0, 2, 2), ("w", 1, 0, 2), ("x", 1, 0, 1), ("w", 1, 2, 2),
+    ("x", 0, 1, 1), ("w", 0, 4, 2), ("x", 1, 1, 1), ("w", 1, 4, 2), ("w", 0, 6, 2), ("w", 1, 6, 2),
+]
+UNITS = [
+    ("w", 0, 0, 2, "V"), ("x", 0, 0, 1, "S"), ("w", 0, 2, 2, "V"), ("w", 1, 0, 2, "S"), ("x", 1, 0, 1, "S"),
+    ("w", 1, 2, 2, "V"), ("x", 0, 1, 1, "S"), ("w", 0, 4, 2, "V"), ("x", 1, 1, 1, "S"), ("w", 1, 4, 2, "V"),
+    ("w", 0, 6, 1, "V"), ("w", 1, 6, 1, "S"), ("w", 0, 7, 1, "S"), ("w", 1, 7, 1, "S"),
+]
+V_EVAC = ((0, 1), (1, 1), (4, 0), (4, 1))
+EVAC_DELAY = 2
+
+
+def tile_mix_hilo_fm_bias_kernel(tc, w, x, b, out):
+    nc = tc.nc
+    with ExitStack() as ctx:
+        keep = ctx.enter_context(tc.tile_pool(name="keep", bufs=1))
+        psum = ctx.enter_context(tc.psum_pool(name="psum", bufs=1))
+        ctx.enter_context(tc.manual_schedule())
+
+        raw = {}
+        for kind, g, first, count in LOADS:
+            width = 128 * count if kind == "w" else N_T
+            c0 = 128 * first if kind == "w" else N_T * first
+            t = keep.tile([P, 4, width], F32, name=f"raw_{kind}{g}_{first}", align_bytes=64)
+            src = w if kind == "w" else x
+            nc.sync.dma_start(
+                out=t[:],
+                in_=src[g * K_PASS : (g + 1) * K_PASS, c0 : c0 + width].rearrange("(p j) c -> p j c", j=4),
+            )
+            for i in range(count):
+                raw[(kind, g, first + i)] = (t, 128 * i)
+
+        b_rows = keep.tile([P, 32], F32, name="b_rows", align_bytes=64)
+        bias = keep.tile([P, 32], F32, name="bias", align_bytes=64)
+        nc.vector.memset(b_rows[:], 0.0)
+        b_view = b.rearrange("(m q c) -> m q c", q=4, c=32)
+        for q in range(4):
+            nc.scalar.dma_start(out=b_rows[32 * q : 32 * q + 8, :], in_=b_view[:, q, :])
+
+        warm = keep.tile([P, 1], F32, name="warm")
+        nc.vector.memset(warm[:], 0.0)
+        nc.scalar.activation(out=warm[:], in_=warm[:], func=ACT.Identity)
+
+        def width_of(u):
+            return 128 * UNITS[u][3] if UNITS[u][0] == "w" else N_T
+
+        def by4(flat):
+            return flat.rearrange("p (c i j) -> p c j i", i=4, j=4)
+
+        tops, parts, codes, scales = {}, {}, {}, {}
+
+        def raw4(u, step):
+            kind, g, first, count, eng = UNITS[u]
+            t, off = raw[(kind, g, first)]
+            n = width_of(u)
+            if step == 1:
+                return t[:, :, off : off + n].rearrange("p j (c i) -> p c j i", i=4)
+            v = t[:].bitcast(BF16)[:, :, 2 * off : 2 * (off + n)]
+            return v.rearrange("p j (c i s) -> p c j i s", i=4, s=2)[:, :, :, :, 1]
+
+        def stage_copy(u):
+            kind, g, first, count, eng = UNITS[u]
+            n = width_of(u)
+            if kind == "w":
+                dst = keep.tile([P, 4 * n], BF16, name=f"top{u}", align_bytes=64)
+                src = raw4(u, 2)
+            else:
+                dst = keep.tile([P, 4 * n], BF16, name=f"xb{u}", align_bytes=64)
+                src = raw4(u, 1)
+            tops[u] = dst
+            if eng == "V":
+                nc.vector.tensor_copy(out=by4(dst[:]), in_=src)
+            else:
+                nc.scalar.copy(out=by4(dst[:]), in_=src)
+
+        def stage_mask(u):
+            if UNITS[u][0] != "w":
+                return
+            n = width_of(u)
+            parts[u] = keep.tile([P, 2, 4 * n], BF16, name=f"parts{u}", align_bytes=64)
+            nc.vector.tensor_scalar(
+                out=parts[u][:, 0, :].bitcast(I32), in0=tops[u][:].bitcast(I32),
+                scalar1=MASK, scalar2=None, op0=ALU.bitwise_and,
+            )
+
+        def stage_low(u):
+            if UNITS[u][0] != "w":
+                return
+            nc.vector.tensor_tensor(
+                out=by4(parts[u][:, 1, :]), in0=raw4(u, 1), in1=by4(parts[u][:, 0, :]), op=ALU.subtract,
+            )
+
+        def stage_quant(u):
+            n = width_of(u)
+            if UNITS[u][0] == "w":
+                src, total = parts[u][:].rearrange("p s e -> p (s e)"), 2 * n
+            else:
+                src, total = tops[u][:], n
+            codes[u] = keep.tile([P, total], U32, name=f"codes{u}", align_bytes=64)
+            scales[u] = keep.tile([P, total], U8, name=f"scales{u}", align_bytes=64)
+            nc.vector.quantize_mx(out=codes[u][:].bitcast(FP8X4), scales=scales[u][:], in_=src)
+
+        wq, xq = {}, {}
+        acc, seen, closed = {}, {}, []
+        free = list(range(8))
+        res = {}
+
+        def stage_passes(u):
+            kind, g, first, count, eng = UNITS[u]
+            todo = []
+            if kind == "w":
+                for i in range(count):
+                    wq[(g, first + i)] = (u, 128 * i)
+                for i in range(count):
+                    for h in range(2):
+                        if (g, h) in xq:
+                            todo.append((first + i, h))
+            else:
+                xq[(g, first)] = u
+                todo = [(m, first) for m in range(8) if (g, m) in wq]
+            for m, h in todo:
+                if (m, h) not in acc:
+                    k = free.pop(0)
+                    acc[(m, h)] = (psum.tile([P, N_T], F32, name=f"bank{k}"), k)
+                    seen[(m, h)] = 0
+                bank = acc[(m, h)][0]
+                wu, off = wq[(g, m)]
+                xu = xq[(g, h)]
+                n = width_of(wu)
+                for part in range(2):
+                    cols = slice(part * n + off, part * n + off + 128)
+                    nc.tensor.matmul_mx(
+                        out=bank[:],
+                        lhsT=codes[wu][:, cols].bitcast(FP8X4),
+                        lhsT_scale=scales[wu][:, cols],
+                        rhs=codes[xu][:].bitcast(FP8X4),
+                        rhs_scale=scales[xu][:],
+                        start=(seen[(m, h)] == 0),
+                        stop=(seen[(m, h)] == 3),
+                    )
+                    seen[(m, h)] += 1
+                if seen[(m, h)] == 4:
+                    closed.append((u, m, h))
+
+        def stage_out(upto):
+            while closed and closed[0][0] <= upto:
+                u, m, h = closed.pop(0)
+                bank, k = acc[(m, h)]
+                r = keep.tile([P, N_T], F32, name=f"res{m}_{h}", align_bytes=64)
+                if (m, h) in V_EVAC:
+                    nc.vector.tensor_scalar(out=r[:], in0=bank[:], scalar1=bias[:, m : m + 1], scalar2=None, op0=ALU.add)
+                else:
+                    nc.scalar.activation(out=r[:], in_=bank[:], func=ACT.Identity, bias=bias[:, m : m + 1])
+                free.append(k)
+                nc.sync.dma_start(out=out[128 * m : 128 * (m + 1), N_T * h : N_T * (h + 1)], in_=r[:])
+
+        n_units = len(UNITS)
+        for s in range(n_units + 3):
+            if s < n_units:
+                stage_copy(s)
+            if s == 4:
+                nc.vector.transpose(out=bias[:], in_=b_rows[:])
+            stage_out(s - 2 - EVAC_DELAY)
+            if 0 <= s - 1 < n_units:
+                stage_mask(s - 1)
+            if 0 <= s - 2 < n_units:
+                stage_quant(s - 2)
+            if 0 <= s - 1 < n_units:
+                stage_low(s - 1)
+            if 0 <= s - 2 < n_units:
+                stage_passes(s - 2)
+        stage_out(n_units)

@@ -15,20 +15,25 @@ FLOPS = 2 * 2 * 1024 * 1024 * 1024
 
 P = 128
 K_PASS = 512
+RUN = 2
 N_T = 512
 MASK = 0xFFF0FFF0 - (1 << 32)
 
 LOADS = [
-    ("w", 0, 0, 2), ("x", 0, 0, 1), ("w", 0, 2, 2), ("w", 1, 0, 2), ("x", 1, 0, 1), ("w", 1, 2, 2),
-    ("x", 0, 1, 1), ("w", 0, 4, 2), ("x", 1, 1, 1), ("w", 1, 4, 2), ("w", 0, 6, 2), ("w", 1, 6, 2),
+    ("w", 0, 0, 2), ("x", 0, 0, 1), ("w", 0, 2, 2), ("x", 0, 1, 1),
+    ("w", 1, 0, 2), ("x", 1, 0, 1), ("w", 1, 2, 2), ("x", 1, 1, 1),
+    ("w", 0, 4, 2), ("w", 1, 4, 2), ("w", 0, 6, 2), ("w", 1, 6, 2),
 ]
 UNITS = [
-    ("w", 0, 0, 2, "V"), ("x", 0, 0, 1, "S"), ("w", 0, 2, 2, "V"), ("w", 1, 0, 2, "S"), ("x", 1, 0, 1, "S"),
-    ("w", 1, 2, 2, "V"), ("x", 0, 1, 1, "S"), ("w", 0, 4, 2, "V"), ("x", 1, 1, 1, "S"), ("w", 1, 4, 2, "V"),
-    ("w", 0, 6, 1, "V"), ("w", 1, 6, 1, "S"), ("w", 0, 7, 1, "S"), ("w", 1, 7, 1, "S"),
+    ("w", 0, 0, 2, "V"), ("x", 0, 0, 1, "S"), ("w", 0, 2, 2, "V"), ("x", 0, 1, 1, "S"),
+    ("w", 1, 0, 2, "V"), ("x", 1, 0, 1, "S"), ("w", 1, 2, 2, "V"), ("x", 1, 1, 1, "S"),
+    ("w", 0, 4, 2, "V"), ("w", 1, 4, 2, "S"),
+    ("w", 0, 6, 1, "S"), ("w", 1, 6, 1, "S"), ("w", 0, 7, 1, "V"), ("w", 1, 7, 1, "V"),
 ]
-V_EVAC = ((0, 1), (1, 1), (4, 0), (4, 1))
-EVAC_DELAY = 2
+EVAC = {(1, 1): "V", (7, 0): "B", (7, 1): "B"}
+EVAC_DELAY = 1
+WARM = 0
+BIAS_STEP = 4
 
 
 def tile_mix_hilo_fm_bias_kernel(tc, w, x, b, out):
@@ -66,33 +71,29 @@ def tile_mix_hilo_fm_bias_kernel(tc, w, x, b, out):
             return 128 * UNITS[u][3] if UNITS[u][0] == "w" else N_T
 
         def by4(flat):
-            return flat.rearrange("p (c i j) -> p c j i", i=4, j=4)
+            return flat.rearrange("p (c i j) -> p c j i", i=RUN, j=4)
 
         tops, parts, codes, scales = {}, {}, {}, {}
 
-        def raw4(u, step):
+        def raw4(u, step, c0, c1):
             kind, g, first, count, eng = UNITS[u]
             t, off = raw[(kind, g, first)]
-            n = width_of(u)
             if step == 1:
-                return t[:, :, off : off + n].rearrange("p j (c i) -> p c j i", i=4)
-            v = t[:].bitcast(BF16)[:, :, 2 * off : 2 * (off + n)]
-            return v.rearrange("p j (c i s) -> p c j i s", i=4, s=2)[:, :, :, :, 1]
+                return t[:, :, off + c0 : off + c1].rearrange("p j (c i) -> p c j i", i=RUN)
+            v = t[:].bitcast(BF16)[:, :, 2 * (off + c0) : 2 * (off + c1)]
+            return v.rearrange("p j (c i s) -> p c j i s", i=RUN, s=2)[:, :, :, :, 1]
 
         def stage_copy(u):
             kind, g, first, count, eng = UNITS[u]
             n = width_of(u)
-            if kind == "w":
-                dst = keep.tile([P, 4 * n], BF16, name=f"top{u}", align_bytes=64)
-                src = raw4(u, 2)
-            else:
-                dst = keep.tile([P, 4 * n], BF16, name=f"xb{u}", align_bytes=64)
-                src = raw4(u, 1)
+            dst = keep.tile([P, 4 * n], BF16, name=f"top{u}", align_bytes=64)
+            step = 2 if kind == "w" else 1
             tops[u] = dst
-            if eng == "V":
-                nc.vector.tensor_copy(out=by4(dst[:]), in_=src)
-            else:
-                nc.scalar.copy(out=by4(dst[:]), in_=src)
+            cut = {"V": n, "S": 0, "H": n * 5 // 8}[eng]
+            if cut > 0:
+                nc.vector.tensor_copy(out=by4(dst[:, : 4 * cut]), in_=raw4(u, step, 0, cut))
+            if cut < n:
+                nc.scalar.copy(out=by4(dst[:, 4 * cut :]), in_=raw4(u, step, cut, n))
 
         def stage_mask(u):
             if UNITS[u][0] != "w":
@@ -108,86 +109,94 @@ def tile_mix_hilo_fm_bias_kernel(tc, w, x, b, out):
             if UNITS[u][0] != "w":
                 return
             nc.vector.tensor_tensor(
-                out=by4(parts[u][:, 1, :]), in0=raw4(u, 1), in1=by4(parts[u][:, 0, :]), op=ALU.subtract,
+                out=by4(parts[u][:, 1, :]), in0=raw4(u, 1, 0, width_of(u)), in1=by4(parts[u][:, 0, :]), op=ALU.subtract,
             )
 
-        def stage_quant(u):
-            n = width_of(u)
-            if UNITS[u][0] == "w":
-                src, total = parts[u][:].rearrange("p s e -> p (s e)"), 2 * n
-            else:
-                src, total = tops[u][:], n
-            codes[u] = keep.tile([P, total], U32, name=f"codes{u}", align_bytes=64)
-            scales[u] = keep.tile([P, total], U8, name=f"scales{u}", align_bytes=64)
-            nc.vector.quantize_mx(out=codes[u][:].bitcast(FP8X4), scales=scales[u][:], in_=src)
+        def quant(key, src, n):
+            codes[key] = keep.tile([P, n], U32, name=f"codes{key[0]}_{key[1]}", align_bytes=64)
+            scales[key] = keep.tile([P, n], U8, name=f"scales{key[0]}_{key[1]}", align_bytes=64)
+            nc.vector.quantize_mx(out=codes[key][:].bitcast(FP8X4), scales=scales[key][:], in_=src)
 
         wq, xq = {}, {}
         acc, seen, closed = {}, {}, []
         free = list(range(8))
-        res = {}
 
-        def stage_passes(u):
+        def run_pass(u, g, m, h, part):
+            if (m, h) not in acc:
+                k = free.pop(0)
+                acc[(m, h)] = (psum.tile([P, N_T], F32, name=f"bank{k}"), k)
+                seen[(m, h)] = 0
+            wkey, off = wq[(g, m, part)]
+            xkey = xq[(g, h)]
+            nc.tensor.matmul_mx(
+                out=acc[(m, h)][0][:],
+                lhsT=codes[wkey][:, off : off + 128].bitcast(FP8X4),
+                lhsT_scale=scales[wkey][:, off : off + 128],
+                rhs=codes[xkey][:].bitcast(FP8X4),
+                rhs_scale=scales[xkey][:],
+                start=(seen[(m, h)] == 0),
+                stop=(seen[(m, h)] == 3),
+            )
+            seen[(m, h)] += 1
+            if seen[(m, h)] == 4:
+                closed.append((u, m, h))
+
+        def stage_quant_w(u, part):
             kind, g, first, count, eng = UNITS[u]
-            todo = []
-            if kind == "w":
-                for i in range(count):
-                    wq[(g, first + i)] = (u, 128 * i)
-                for i in range(count):
-                    for h in range(2):
-                        if (g, h) in xq:
-                            todo.append((first + i, h))
-            else:
-                xq[(g, first)] = u
-                todo = [(m, first) for m in range(8) if (g, m) in wq]
+            if kind != "w":
+                return
+            n = width_of(u)
+            quant((u, part), parts[u][:, part, :], n)
+            for i in range(count):
+                wq[(g, first + i, part)] = ((u, part), 128 * i)
+            todo = [(first + i, h) for i in range(count) for h in range(2) if (g, h) in xq]
+            todo.sort(key=lambda mh: mh not in acc)
             for m, h in todo:
-                if (m, h) not in acc:
-                    k = free.pop(0)
-                    acc[(m, h)] = (psum.tile([P, N_T], F32, name=f"bank{k}"), k)
-                    seen[(m, h)] = 0
-                bank = acc[(m, h)][0]
-                wu, off = wq[(g, m)]
-                xu = xq[(g, h)]
-                n = width_of(wu)
+                run_pass(u, g, m, h, part)
+
+        def stage_quant_x(u):
+            kind, g, h, count, eng = UNITS[u]
+            if kind != "x":
+                return
+            quant((u, 0), tops[u][:], N_T)
+            xq[(g, h)] = (u, 0)
+            todo = [m for m in range(8) if (g, m, 0) in wq]
+            todo.sort(key=lambda m: (m, h) not in acc)
+            for m in todo:
                 for part in range(2):
-                    cols = slice(part * n + off, part * n + off + 128)
-                    nc.tensor.matmul_mx(
-                        out=bank[:],
-                        lhsT=codes[wu][:, cols].bitcast(FP8X4),
-                        lhsT_scale=scales[wu][:, cols],
-                        rhs=codes[xu][:].bitcast(FP8X4),
-                        rhs_scale=scales[xu][:],
-                        start=(seen[(m, h)] == 0),
-                        stop=(seen[(m, h)] == 3),
-                    )
-                    seen[(m, h)] += 1
-                if seen[(m, h)] == 4:
-                    closed.append((u, m, h))
+                    if (g, m, part) in wq:
+                        run_pass(u, g, m, h, part)
 
         def stage_out(upto):
             while closed and closed[0][0] <= upto:
                 u, m, h = closed.pop(0)
                 bank, k = acc[(m, h)]
                 r = keep.tile([P, N_T], F32, name=f"res{m}_{h}", align_bytes=64)
-                if (m, h) in V_EVAC:
-                    nc.vector.tensor_scalar(out=r[:], in0=bank[:], scalar1=bias[:, m : m + 1], scalar2=None, op0=ALU.add)
-                else:
-                    nc.scalar.activation(out=r[:], in_=bank[:], func=ACT.Identity, bias=bias[:, m : m + 1])
+                eng = EVAC.get((m, h), "S")
+                cut = {"V": N_T, "S": 0, "B": N_T // 2}[eng]
+                if cut < N_T:
+                    nc.scalar.activation(out=r[:, cut:], in_=bank[:, cut:], func=ACT.Identity, bias=bias[:, m : m + 1])
+                if cut > 0:
+                    nc.vector.tensor_scalar(out=r[:, :cut], in0=bank[:, :cut], scalar1=bias[:, m : m + 1], scalar2=None, op0=ALU.add)
                 free.append(k)
                 nc.sync.dma_start(out=out[128 * m : 128 * (m + 1), N_T * h : N_T * (h + 1)], in_=r[:])
 
+        if WARM:
+            warm_bank = psum.tile([P, N_T], F32, name="bank7")
         n_units = len(UNITS)
         for s in range(n_units + 3):
+            i, q = s - 1, s - 2
             if s < n_units:
                 stage_copy(s)
-            if s == 4:
+            if s == BIAS_STEP:
                 nc.vector.transpose(out=bias[:], in_=b_rows[:])
-            stage_out(s - 2 - EVAC_DELAY)
-            if 0 <= s - 1 < n_units:
-                stage_mask(s - 1)
-            if 0 <= s - 2 < n_units:
-                stage_quant(s - 2)
-            if 0 <= s - 1 < n_units:
-                stage_low(s - 1)
-            if 0 <= s - 2 < n_units:
-                stage_passes(s - 2)
+            stage_out(q - EVAC_DELAY)
+            if 0 <= i < n_units:
+                stage_mask(i)
+            if 0 <= q < n_units:
+                stage_quant_w(q, 1)
+                stage_quant_x(q)
+            if 0 <= i < n_units:
+                stage_low(i)
+                stage_quant_w(i, 0)
         stage_out(n_units)

from contextlib import ExitStack

import concourse.mybir as mybir

F32 = mybir.dt.float32
BF16 = mybir.dt.bfloat16
I32 = mybir.dt.int32
U32 = mybir.dt.uint32
U8 = mybir.dt.uint8
FP8X4 = mybir.dt.float8_e4m3fn_x4
ALU = mybir.AluOpType
ACT = mybir.ActivationFunctionType

FLOPS = 2 * 2 * 1024 * 1024 * 1024

P = 128
K_PASS = 512
RUN = 2
N_T = 512
MASK = 0xFFF0FFF0 - (1 << 32)

LOADS = [
    ("w", 0, 0, 2), ("x", 0, 0, 1), ("w", 0, 2, 2), ("x", 0, 1, 1),
    ("w", 1, 0, 2), ("x", 1, 0, 1), ("w", 1, 2, 2), ("x", 1, 1, 1),
    ("w", 0, 4, 2), ("w", 1, 4, 2), ("w", 0, 6, 2), ("w", 1, 6, 2),
]
UNITS = [
    ("w", 0, 0, 2, "V"), ("x", 0, 0, 1, "S"), ("w", 0, 2, 2, "V"), ("x", 0, 1, 1, "S"),
    ("w", 1, 0, 2, "V"), ("x", 1, 0, 1, "S"), ("w", 1, 2, 2, "V"), ("x", 1, 1, 1, "S"),
    ("w", 0, 4, 2, "V"), ("w", 1, 4, 2, "S"),
    ("w", 0, 6, 1, "S"), ("w", 1, 6, 1, "S"), ("w", 0, 7, 1, "V"), ("w", 1, 7, 1, "V"),
]
EVAC = {(1, 1): "V", (7, 0): "B", (7, 1): "B"}
EVAC_DELAY = 1
WARM = 0
BIAS_STEP = 4


def tile_mix_hilo_fm_bias_kernel(tc, w, x, b, out):
    nc = tc.nc
    with ExitStack() as ctx:
        keep = ctx.enter_context(tc.tile_pool(name="keep", bufs=1))
        psum = ctx.enter_context(tc.psum_pool(name="psum", bufs=1))
        ctx.enter_context(tc.manual_schedule())

        raw = {}
        for kind, g, first, count in LOADS:
            width = 128 * count if kind == "w" else N_T
            c0 = 128 * first if kind == "w" else N_T * first
            t = keep.tile([P, 4, width], F32, name=f"raw_{kind}{g}_{first}", align_bytes=64)
            src = w if kind == "w" else x
            nc.sync.dma_start(
                out=t[:],
                in_=src[g * K_PASS : (g + 1) * K_PASS, c0 : c0 + width].rearrange("(p j) c -> p j c", j=4),
            )
            for i in range(count):
                raw[(kind, g, first + i)] = (t, 128 * i)

        b_rows = keep.tile([P, 32], F32, name="b_rows", align_bytes=64)
        bias = keep.tile([P, 32], F32, name="bias", align_bytes=64)
        nc.vector.memset(b_rows[:], 0.0)
        b_view = b.rearrange("(m q c) -> m q c", q=4, c=32)
        for q in range(4):
            nc.scalar.dma_start(out=b_rows[32 * q : 32 * q + 8, :], in_=b_view[:, q, :])

        warm = keep.tile([P, 1], F32, name="warm")
        nc.vector.memset(warm[:], 0.0)
        nc.scalar.activation(out=warm[:], in_=warm[:], func=ACT.Identity)

        def width_of(u):
            return 128 * UNITS[u][3] if UNITS[u][0] == "w" else N_T

        def by4(flat):
            return flat.rearrange("p (c i j) -> p c j i", i=RUN, j=4)

        tops, parts, codes, scales = {}, {}, {}, {}

        def raw4(u, step, c0, c1):
            kind, g, first, count, eng = UNITS[u]
            t, off = raw[(kind, g, first)]
            if step == 1:
                return t[:, :, off + c0 : off + c1].rearrange("p j (c i) -> p c j i", i=RUN)
            v = t[:].bitcast(BF16)[:, :, 2 * (off + c0) : 2 * (off + c1)]
            return v.rearrange("p j (c i s) -> p c j i s", i=RUN, s=2)[:, :, :, :, 1]

        def stage_copy(u):
            kind, g, first, count, eng = UNITS[u]
            n = width_of(u)
            dst = keep.tile([P, 4 * n], BF16, name=f"top{u}", align_bytes=64)
            step = 2 if kind == "w" else 1
            tops[u] = dst
            cut = {"V": n, "S": 0, "H": n * 5 // 8}[eng]
            if cut > 0:
                nc.vector.tensor_copy(out=by4(dst[:, : 4 * cut]), in_=raw4(u, step, 0, cut))
            if cut < n:
                nc.scalar.copy(out=by4(dst[:, 4 * cut :]), in_=raw4(u, step, cut, n))

        def stage_mask(u):
            if UNITS[u][0] != "w":
                return
            n = width_of(u)
            parts[u] = keep.tile([P, 2, 4 * n], BF16, name=f"parts{u}", align_bytes=64)
            nc.vector.tensor_scalar(
                out=parts[u][:, 0, :].bitcast(I32), in0=tops[u][:].bitcast(I32),
                scalar1=MASK, scalar2=None, op0=ALU.bitwise_and,
            )

        def stage_low(u):
            if UNITS[u][0] != "w":
                return
            nc.vector.tensor_tensor(
                out=by4(parts[u][:, 1, :]), in0=raw4(u, 1, 0, width_of(u)), in1=by4(parts[u][:, 0, :]), op=ALU.subtract,
            )

        def quant(key, src, n):
            codes[key] = keep.tile([P, n], U32, name=f"codes{key[0]}_{key[1]}", align_bytes=64)
            scales[key] = keep.tile([P, n], U8, name=f"scales{key[0]}_{key[1]}", align_bytes=64)
            nc.vector.quantize_mx(out=codes[key][:].bitcast(FP8X4), scales=scales[key][:], in_=src)

        wq, xq = {}, {}
        acc, seen, closed = {}, {}, []
        free = list(range(8))

        def run_pass(u, g, m, h, part):
            if (m, h) not in acc:
                k = free.pop(0)
                acc[(m, h)] = (psum.tile([P, N_T], F32, name=f"bank{k}"), k)
                seen[(m, h)] = 0
            wkey, off = wq[(g, m, part)]
            xkey = xq[(g, h)]
            nc.tensor.matmul_mx(
                out=acc[(m, h)][0][:],
                lhsT=codes[wkey][:, off : off + 128].bitcast(FP8X4),
                lhsT_scale=scales[wkey][:, off : off + 128],
                rhs=codes[xkey][:].bitcast(FP8X4),
                rhs_scale=scales[xkey][:],
                start=(seen[(m, h)] == 0),
                stop=(seen[(m, h)] == 3),
            )
            seen[(m, h)] += 1
            if seen[(m, h)] == 4:
                closed.append((u, m, h))

        def stage_quant_w(u, part):
            kind, g, first, count, eng = UNITS[u]
            if kind != "w":
                return
            n = width_of(u)
            quant((u, part), parts[u][:, part, :], n)
            for i in range(count):
                wq[(g, first + i, part)] = ((u, part), 128 * i)
            todo = [(first + i, h) for i in range(count) for h in range(2) if (g, h) in xq]
            todo.sort(key=lambda mh: mh not in acc)
            for m, h in todo:
                run_pass(u, g, m, h, part)

        def stage_quant_x(u):
            kind, g, h, count, eng = UNITS[u]
            if kind != "x":
                return
            quant((u, 0), tops[u][:], N_T)
            xq[(g, h)] = (u, 0)
            todo = [m for m in range(8) if (g, m, 0) in wq]
            todo.sort(key=lambda m: (m, h) not in acc)
            for m in todo:
                for part in range(2):
                    if (g, m, part) in wq:
                        run_pass(u, g, m, h, part)

        def stage_out(upto):
            while closed and closed[0][0] <= upto:
                u, m, h = closed.pop(0)
                bank, k = acc[(m, h)]
                r = keep.tile([P, N_T], F32, name=f"res{m}_{h}", align_bytes=64)
                eng = EVAC.get((m, h), "S")
                cut = {"V": N_T, "S": 0, "B": N_T // 2}[eng]
                if cut < N_T:
                    nc.scalar.activation(out=r[:, cut:], in_=bank[:, cut:], func=ACT.Identity, bias=bias[:, m : m + 1])
                if cut > 0:
                    nc.vector.tensor_scalar(out=r[:, :cut], in0=bank[:, :cut], scalar1=bias[:, m : m + 1], scalar2=None, op0=ALU.add)
                free.append(k)
                nc.sync.dma_start(out=out[128 * m : 128 * (m + 1), N_T * h : N_T * (h + 1)], in_=r[:])

        if WARM:
            warm_bank = psum.tile([P, N_T], F32, name="bank7")
        n_units = len(UNITS)
        for s in range(n_units + 3):
            i, q = s - 1, s - 2
            if s < n_units:
                stage_copy(s)
            if s == BIAS_STEP:
                nc.vector.transpose(out=bias[:], in_=b_rows[:])
            stage_out(q - EVAC_DELAY)
            if 0 <= i < n_units:
                stage_mask(i)
            if 0 <= q < n_units:
                stage_quant_w(q, 1)
                stage_quant_x(q)
            if 0 <= i < n_units:
                stage_low(i)
                stage_quant_w(i, 0)
        stage_out(n_units)
